import numpy as np
import ml_dtypes


def mxq(x, axis, fmt="e4m3"):
    dtype, down = {"e4m3": (ml_dtypes.float8_e4m3fn, 7), "e5m2": (ml_dtypes.float8_e5m2, 14)}[fmt]
    v = np.moveaxis(np.asarray(x, np.float32).astype(ml_dtypes.bfloat16).astype(np.float64), axis, -1)
    blocks = v.reshape(v.shape[:-1] + (-1, 32))
    amax = np.abs(blocks).max(-1, keepdims=True)
    byte = np.maximum(np.where(amax > 0, np.frexp(amax)[1] - 1 + 127, 0) - down, 1)
    scale = np.exp2(byte - 127.0)
    codes = (blocks / scale).astype(np.float32).astype(dtype).astype(np.float64)
    return np.moveaxis((codes * scale).reshape(v.shape), -1, axis)


WIDE = False


def mx_kscale(k):
    if not WIDE:
        return np.ones(k)
    levels = np.array([10, -10, 5, -5, 0])
    if k % 512:
        return np.exp2(np.random.permutation(np.resize(levels, k // 32))).repeat(32)
    a = np.empty((k // 512, 16))
    for p in range(k // 512):
        a[p, :8] = np.random.permutation(np.resize(levels, 8))
        for g in range(8):
            far = levels[np.abs(levels - a[p, g]) >= 10]
            a[p, g + 8] = far[np.random.randint(len(far))]
    return np.exp2(a.ravel()).repeat(32)


def f64(x):
    return np.asarray(x).astype(np.float64)


def striped(idx):
    return np.tile(np.asarray(idx).reshape(-1, 16).T, (8, 1)).astype(np.uint16)


def unstriped(offs):
    return offs[:16].T.reshape(-1).astype(np.int64)


def striped8(idx):
    return np.asarray(idx).reshape(8, -1, 16).transpose(0, 2, 1).reshape(128, -1).astype(np.uint16)


def unstriped8(offs):
    return offs.reshape(8, 16, -1).transpose(0, 2, 1).reshape(8, -1).astype(np.int64)


def pick8(x, idx, run):
    r = np.arange(len(x))
    return x[r[:, None], idx[r % (8 * run) // run]]


E2M1 = np.array([0.0, 0.5, 1.0, 1.5, 2.0, 3.0, 4.0, 6.0, -0.0, -0.5, -1.0, -1.5, -2.0, -3.0, -4.0, -6.0])


def pack_weight(w, fmt):
    k, n = w.shape
    w = f64(np.asarray(w, np.float32).astype(ml_dtypes.bfloat16)).reshape(k // 32, 32, n)
    amax = np.abs(w).max(1)
    if fmt == "e4m3":
        byte = np.frexp(amax)[1] - 1 + 127 - 7
    else:
        mant, ex = np.frexp(amax / 6.0)
        byte = np.where(mant > 0.5, ex, ex - 1) + 127
    byte = np.clip(np.where(amax > 0, byte, 1), 1, 254)
    scaled = (w * np.exp2(127.0 - byte)[:, None, :]).reshape(k, n).astype(np.float32)
    by_word = np.ascontiguousarray(scaled.reshape(k // 512, 128, 4, n).transpose(0, 1, 3, 2))
    if fmt == "e4m3":
        words = by_word.astype(ml_dtypes.float8_e4m3fn).view(np.uint8)
    else:
        c = by_word.astype(ml_dtypes.float4_e2m1fn).view(np.uint8) & 0xF
        words = (c[..., 0::2] | (c[..., 1::2] << 4)).reshape(k // 512, 128, 2 * n)
    return np.ascontiguousarray(words), np.ascontiguousarray(byte.astype(np.uint8).reshape(k // 512, 16, n))


def unpack_weight(words, scales, fmt):
    g, _, n = scales.shape
    words = np.ascontiguousarray(words).reshape(g, 128, n, -1)
    if fmt == "e4m3":
        vals = words.view(ml_dtypes.float8_e4m3fn).astype(np.float64)
    else:
        nib = np.empty((g, 128, n, 4), np.uint8)
        nib[..., 0::2] = words & 0xF
        nib[..., 1::2] = words >> 4
        vals = E2M1[nib]
    vals = vals * np.repeat(np.exp2(scales.astype(np.float64) - 127.0), 8, axis=1)[..., None]
    return vals.transpose(0, 1, 3, 2).reshape(g * 512, n)


K, J, R, T, Z, M, C, O, N, U = 512, 512, 512, 2048, 512, 1024, 1024, 512, 256, 1024


def setup_inputs():
    n = np.random.standard_normal
    idx = np.random.permutation(T)[:J]
    idx2 = np.random.permutation(M)[:J]
    idx3 = np.stack([np.random.permutation(C)[:J] for _ in range(8)])
    idx4 = np.stack([np.random.permutation(C)[:J] for _ in range(8)])
    idx5 = np.stack([np.random.permutation(C)[:O] for _ in range(8)])
    idx6 = np.stack([np.random.permutation(U)[:O] for _ in range(8)])
    idx7 = np.stack([np.random.permutation(U)[:O] for _ in range(8)])
    fk = mx_kscale(K)
    fz = mx_kscale(Z)
    fr = mx_kscale(R)
    xtp = pack_weight(n((K, T)) * fk[:, None], "e2m1")
    wp = pack_weight(n((K, R)) * 1 / np.sqrt(K) / fk[:, None], "e4m3")
    xop = pack_weight(n((Z, M)) / fz[:, None], "e4m3")
    w2p = pack_weight(n((Z, R)) * 1 / np.sqrt(Z) * fz[:, None], "e2m1")
    wbp = pack_weight(n((R, N)) * 1 / np.sqrt(R) / fr[:, None], "e2m1")
    return {
        "xt_words": xtp[0],
        "xt_scales": xtp[1],
        "w_words": wp[0],
        "w_scales": wp[1],
        "xo_words": xop[0],
        "xo_scales": xop[1],
        "w2_words": w2p[0],
        "w2_scales": w2p[1],
        "sa": (np.random.uniform(0.5, 1.6, (R, 1)) * fr[:, None]).astype(np.float32),
        "wb_words": wbp[0],
        "wb_scales": wbp[1],
        "offs": striped(idx),
        "offs2": striped(idx2),
        "offs3": striped8(idx3),
        "offs4": striped8(idx4),
        "offs5": striped8(idx5),
        "offs6": striped8(idx6),
        "offs7": striped8(idx7),
    }


def reference(xt_words, xt_scales, w_words, w_scales, xo_words, xo_scales, w2_words, w2_scales, sa, wb_words, wb_scales, offs, offs2, offs3, offs4, offs5, offs6, offs7):
    idx = unstriped(offs)
    idx2 = unstriped(offs2)
    idx3 = unstriped8(offs3)
    idx4 = unstriped8(offs4)
    idx5 = unstriped8(offs5)
    idx6 = unstriped8(offs6)
    idx7 = unstriped8(offs7)
    xtu = unpack_weight(xt_words, xt_scales, "e2m1")
    wu = unpack_weight(w_words, w_scales, "e4m3")
    xou = unpack_weight(xo_words, xo_scales, "e4m3")
    w2u = unpack_weight(w2_words, w2_scales, "e2m1")
    wbu = unpack_weight(wb_words, wb_scales, "e2m1")
    xtidxg = xtu[:, idx]
    a = wu.T @ xtidxg
    xoidx2g = xou[:, idx2]
    b = w2u.T @ xoidx2g
    pw = np.zeros((R, C))
    pw[np.arange(R)[:, None], idx3[np.arange(R) % 512 // 64]] = a
    pv = np.zeros((R, C))
    pv[np.arange(R)[:, None], idx4[np.arange(R) % 512 // 64]] = b
    pg = np.maximum(pw, pv)
    pm = np.mean(np.abs(pg), axis=1, keepdims=True)
    ql = f64(sa) / pm
    hid = pick8(pg, idx5, 64) * ql
    hidq = mxq(hid, 0, "e4m3")
    p = wbu.T @ hidq
    m0 = np.maximum(p, 0.0)
    m1 = np.maximum(-p, 0.0)
    m2 = np.zeros((N, U))
    m2[np.arange(N)[:, None], idx6[np.arange(N) % 128 // 16]] = m0
    m3 = np.zeros((N, U))
    m3[np.arange(N)[:, None], idx7[np.arange(N) % 128 // 16]] = m1
    y = m2 - m3
    return y

@@ -1,0 +1,232 @@
+from contextlib import ExitStack
+
+import concourse.mybir as mybir
+
+K, J, R, T, Z, M, C, O, N, U = 512, 512, 512, 2048, 512, 1024, 1024, 512, 256, 1024
+FLOPS = 2 * K * R * J + 2 * Z * R * J + 2 * R * N * O
+
+F32 = mybir.dt.float32
+BF16 = mybir.dt.bfloat16
+I32 = mybir.dt.int32
+U32 = mybir.dt.uint32
+U16 = mybir.dt.uint16
+U8 = mybir.dt.uint8
+E4M3 = mybir.dt.float8_e4m3fn_x4
+E2M1 = mybir.dt.float4_e2m1fn_x4
+ALU = mybir.AluOpType
+COPY = mybir.ActivationFunctionType.Copy
+
+P = 128
+PACK = 4
+QUADS = 4
+HALF = O // 2
+
+
+def tile_picked_tokens_bare_two_levelled_one_endsplit_kernel(
+    tc, xt_words, xt_scales, w_words, w_scales, xo_words, xo_scales, w2_words, w2_scales, sa,
+    wb_words, wb_scales, offs, offs2, offs3, offs4, offs5, offs6, offs7, out,
+):
+    nc = tc.nc
+
+    with ExitStack() as ctx:
+        lists = ctx.enter_context(tc.tile_pool(name="lists", bufs=1))
+        keep = ctx.enter_context(tc.tile_pool(name="keep", bufs=1))
+        psum = ctx.enter_context(tc.psum_pool(name="psum", bufs=8))
+
+        def load_list(src, name):
+            t = lists.tile([P, J // 16], U16, name=name)
+            nc.sync.dma_start(t[:], src)
+            return t
+
+        def entries(lst, lo, hi):
+            return lst[:, lo // 16 : hi // 16]
+
+        def load_words(src, dtype, width, name):
+            t = keep.tile([P, width], dtype, name=name, align_bytes=64)
+            nc.sync.dma_start(t[:].bitcast(I32), src.bitcast(I32))
+            return t
+
+        def stage_scales(src, width, name):
+            rows = keep.tile([PACK, QUADS, width // 4], I32, name=name)
+            nc.sync.dma_start(rows[:], src[0].rearrange("(q i) n -> i q n", i=PACK).bitcast(I32))
+            return rows
+
+        def zeroed_plane(width, name):
+            plane = keep.tile([P, width], U8, name=name, align_bytes=64)
+            nc.vector.memset(plane[:].bitcast(I32), 0)
+            return plane
+
+        def spread_scales(plane, rows):
+            for q in range(QUADS):
+                nc.vector.tensor_copy(plane[32 * q : 32 * q + PACK, :].bitcast(I32), rows[:, q, :])
+
+        def load_scales(plane, src):
+            for q in range(QUADS):
+                nc.sync.dma_start(
+                    plane[32 * q : 32 * q + PACK, :].bitcast(I32),
+                    src[0, PACK * q : PACK * (q + 1), :].bitcast(I32),
+                )
+
+        def dealt(src):
+            return src[:].rearrange("p (m t) -> p t m", t=PACK)
+
+        def board(name, tag, engine=nc.gpsimd):
+            t = keep.tile([P, C], F32, name=name, tag=tag)
+            engine.memset(t[:], 0.0)
+            return t
+
+        def scatter(window, lst, lo, hi, values):
+            nc.scalar.activation(window[:].indirect(entries(lst, lo, hi)), values, COPY)
+
+        xo_rows = stage_scales(xo_scales, M, "xo_rows")
+        w2_rows = stage_scales(w2_scales, R, "w2_rows")
+        idx2 = load_list(offs2, "idx2")
+        w2_raw = load_words(w2_words[0], U16, R, "w2_raw")
+        xo_table = load_words(xo_words[0].rearrange("p n t -> p (n t)"), U32, M, "xo_table")
+        idx4 = load_list(offs4, "idx4")
+        idx1 = load_list(offs, "idx1")
+        xt_table = load_words(xt_words[0], U16, T, "xt_table")
+        w_raw = load_words(w_words[0].rearrange("p n t -> p (n t)"), I32, R, "w_raw")
+
+        xo_plane = zeroed_plane(M, "xo_plane")
+        w2_plane_raw = zeroed_plane(R, "w2_plane_raw")
+        xt_plane = zeroed_plane(T, "xt_plane")
+        w_plane_raw = zeroed_plane(R, "w_plane_raw")
+        wb_plane = zeroed_plane(N, "wb_plane")
+        pv = [board("pv0", "pv0", nc.vector), board("pv1", "pv1")]
+
+        spread_scales(xo_plane, xo_rows)
+        spread_scales(w2_plane_raw, w2_rows)
+        w2_plane = keep.tile([P, PACK, P], U8, name="w2_plane", align_bytes=64)
+        nc.vector.tensor_copy(w2_plane[:, :2, :], dealt(w2_plane_raw)[:, :2, :])
+        w2_codes = keep.tile([P, PACK, P], U16, name="w2_codes", align_bytes=64)
+        nc.scalar.copy(w2_codes[:], dealt(w2_raw))
+        xo_codes = keep.tile([P, J], U32, name="xo_codes", align_bytes=64)
+        xo_bytes = keep.tile([P, J], U8, name="xo_bytes", align_bytes=64)
+
+        def product_b(t, lo, hi):
+            acc = psum.tile([P, J], F32, name="acc")
+            nc.tensor.matmul_mx(
+                acc[:, lo:hi], lhsT=w2_codes[:, t, :].bitcast(E2M1), lhsT_scale=w2_plane[:, t, :],
+                rhs=xo_codes[:, lo:hi].bitcast(E4M3), rhs_scale=xo_bytes[:, lo:hi], start=True, stop=True,
+            )
+            vals = keep.tile([P, hi - lo], F32, name="b%d_%d" % (t, lo), tag="b%d_%d" % (t, lo))
+            nc.vector.tensor_copy(vals[:], acc[:, lo:hi])
+            scatter(pv[t], idx4, lo, hi, vals[:])
+
+        for lo, hi in ((0, 128), (128, 256), (256, 512)):
+            nc.vector.tensor_copy(xo_bytes[:, lo:hi], xo_plane[:].indirect(entries(idx2, lo, hi)))
+            nc.vector.tensor_copy(xo_codes[:, lo:hi], xo_table[:].indirect(entries(idx2, lo, hi)))
+            for t in range(2):
+                product_b(t, lo, hi)
+        nc.vector.tensor_copy(w2_plane[:, 2:, :], dealt(w2_plane_raw)[:, 2:, :])
+        pv.append(board("pv2", "b0_128"))
+        product_b(2, 0, J)
+        pv.append(board("pv3", "b0_256"))
+        product_b(3, 0, J)
+
+        load_scales(xt_plane, xt_scales)
+        load_scales(w_plane_raw, w_scales)
+        idx3 = load_list(offs3, "idx3")
+        sa_rows = keep.tile([P, PACK], F32, name="sa_rows")
+        nc.sync.dma_start(sa_rows[:], sa.rearrange("(p t) o -> p (t o)", t=PACK))
+        idx5 = load_list(offs5, "idx5")
+        wb_codes = load_words(wb_words[0], U16, N, "wb_codes")
+        load_scales(wb_plane, wb_scales)
+        idx6 = load_list(offs6, "idx6")
+        idx7 = load_list(offs7, "idx7")
+
+        w_codes = keep.tile([P, PACK, P], I32, name="w_codes", align_bytes=64)
+        nc.vector.tensor_copy(w_codes[:], dealt(w_raw))
+        w_plane = keep.tile([P, PACK, P], U8, name="w_plane", align_bytes=64)
+        nc.vector.tensor_copy(w_plane[:], dealt(w_plane_raw))
+        xt_codes = keep.tile([P, J], U16, name="xt_codes", align_bytes=64)
+        nc.vector.tensor_copy(xt_codes[:], xt_table[:].indirect(idx1[:]))
+        xt_bytes = keep.tile([P, J], U8, name="xt_bytes", align_bytes=64)
+        nc.vector.tensor_copy(xt_bytes[:], xt_plane[:].indirect(idx1[:]))
+
+        a_vals = []
+        for t in range(PACK):
+            acc = psum.tile([P, J], F32, name="acc")
+            nc.tensor.matmul_mx(
+                acc[:], lhsT=w_codes[:, t, :].bitcast(E4M3), lhsT_scale=w_plane[:, t, :],
+                rhs=xt_codes[:].bitcast(E2M1), rhs_scale=xt_bytes[:], start=True, stop=True,
+            )
+            vals = keep.tile([P, J], F32, name="a%d" % t, tag="a%d" % t)
+            nc.vector.tensor_copy(vals[:], acc[:])
+            a_vals.append(vals)
+        pw = []
+        for t, tag in enumerate(("b1_256", "b2_0", "b3_0", "a0")):
+            pw.append(board("pw%d" % t, tag))
+            scatter(pw[t], idx3, 0, J, a_vals[t][:])
+
+        pg, ql = [], []
+        for t in range(PACK):
+            g = keep.tile([P, C], F32, name="pg%d" % t)
+            nc.vector.tensor_tensor(g[:], pw[t][:], pv[t][:], ALU.max)
+            total = keep.tile([P, 1], F32, name="total%d" % t)
+            nc.vector.tensor_reduce(total[:], g[:], mybir.AxisListType.X, ALU.add, apply_absolute_value=True)
+            inv = keep.tile([P, 1], F32, name="inv%d" % t, tag="inv%d" % t)
+            nc.vector.reciprocal(inv[:], total[:])
+            q = keep.tile([P, 1], F32, name="ql%d" % t)
+            nc.vector.tensor_scalar(q[:], inv[:], sa_rows[:, t : t + 1], float(C), ALU.mult, ALU.mult)
+            pg.append(g)
+            ql.append(q)
+
+        m2 = [board("m2_0", "pv0"), board("m2_1", "pv1")]
+        m3 = [board("m3_0", "b1_256"), board("m3_1", "b2_0")]
+
+        def fetch(dst, t, h):
+            nc.scalar.activation(dst, pg[t][:].indirect(entries(idx5, h * HALF, (h + 1) * HALF)), COPY, scale=ql[t][:])
+
+        hid_codes = keep.tile([P, O], U32, name="hid_codes", align_bytes=64)
+        hid_bytes = keep.tile([P, O], U8, name="hid_bytes", align_bytes=64)
+
+        def quantise(planes, h):
+            woven = keep.tile([P, HALF, PACK], BF16, name="woven%d" % h, align_bytes=64)
+            nc.vector.tensor_copy(
+                woven[:].rearrange("p (c i) t -> p c t i", i=4), planes[:].rearrange("p t (c i) -> p c t i", i=4)
+            )
+            cols = slice(h * HALF, (h + 1) * HALF)
+            nc.vector.quantize_mx(hid_codes[:, cols].bitcast(E4M3), hid_bytes[:, cols], woven[:].rearrange("p c t -> p (c t)"))
+
+        def product_p(acc, u, h):
+            cols = slice(h * HALF, (h + 1) * HALF)
+            nc.tensor.matmul_mx(
+                acc[:, cols], lhsT=wb_codes[:, u * P : (u + 1) * P].bitcast(E2M1), lhsT_scale=wb_plane[:, u * P : (u + 1) * P],
+                rhs=hid_codes[:, cols].bitcast(E4M3), rhs_scale=hid_bytes[:, cols], start=True, stop=True,
+            )
+
+        def split_and_scatter(acc, u, lo, hi):
+            pos = keep.tile([P, hi - lo], F32, name="m0_%d_%d" % (u, lo))
+            nc.vector.tensor_scalar(pos[:], acc[:, lo:hi], 0.0, None, ALU.max)
+            scatter(m2[u], idx6, lo, hi, pos[:])
+            neg = keep.tile([P, hi - lo], F32, name="m1_%d_%d" % (u, lo))
+            nc.vector.tensor_scalar(neg[:], acc[:, lo:hi], -1.0, 0.0, ALU.mult, ALU.max)
+            scatter(m3[u], idx7, lo, hi, neg[:])
+
+        planes0 = keep.tile([P, PACK, HALF], BF16, name="planes0")
+        for t in range(PACK):
+            fetch(planes0[:, t, :], t, 0)
+        planes1 = keep.tile([P, PACK, HALF], BF16, name="planes1", tag="inv%d" % (PACK - 1))
+        for t in range(PACK):
+            fetch(planes1[:, t, :], t, 1)
+
+        last = psum.tile([P, O], F32, name="acc")
+        for h, planes in enumerate((planes0, planes1)):
+            quantise(planes, h)
+            acc = psum.tile([P, O], F32, name="acc")
+            product_p(acc, 0, h)
+            product_p(last, 1, h)
+            split_and_scatter(acc, 0, h * HALF, (h + 1) * HALF)
+        split_and_scatter(last, 1, 0, O)
+
+        def finish(u, lo, hi, queue):
+            y = keep.tile([P, hi - lo], F32, name="y%d_%d" % (u, lo))
+            nc.vector.tensor_tensor(y[:], m2[u][:, lo:hi], m3[u][:, lo:hi], ALU.subtract)
+            queue.dma_start(out[u * P : (u + 1) * P, lo:hi], y[:])
+
+        finish(0, 0, U, nc.sync)
+        finish(1, 0, 512, nc.sync)
+        finish(1, 512, 768, nc.scalar)
+        finish(1, 768, U, nc.sync)

@@ -51,9 +51,9 @@ def tile_picked_tokens_bare_two_levelled_one_endsplit_kernel(
             nc.sync.dma_start(rows[:], src[0].rearrange("(q i) n -> i q n", i=PACK).bitcast(I32))
             return rows
 
-        def zeroed_plane(width, name):
-            plane = keep.tile([P, width], U8, name=name, align_bytes=64)
-            nc.vector.memset(plane[:].bitcast(I32), 0)
+        def zeroed_plane(width, name, tag, engine):
+            plane = keep.tile([P, width], U8, name=name, tag=tag, align_bytes=64)
+            engine.memset(plane[:].bitcast(I32), 0)
             return plane
 
         def spread_scales(plane, rows):
@@ -71,7 +71,7 @@ def tile_picked_tokens_bare_two_levelled_one_endsplit_kernel(
             return src[:].rearrange("p (m t) -> p t m", t=PACK)
 
         def board(name, tag, engine=nc.gpsimd):
-            t = keep.tile([P, C], F32, name=name, tag=tag)
+            t = keep.tile([P, C], F32, name=name, tag=tag, align_bytes=64)
             engine.memset(t[:], 0.0)
             return t
 
@@ -83,53 +83,66 @@ def tile_picked_tokens_bare_two_levelled_one_endsplit_kernel(
         idx2 = load_list(offs2, "idx2")
         w2_raw = load_words(w2_words[0], U16, R, "w2_raw")
         xo_table = load_words(xo_words[0].rearrange("p n t -> p (n t)"), U32, M, "xo_table")
+        sa_rows = keep.tile([P, PACK], F32, name="sa_rows", tag="sa_rows", align_bytes=64)
+        nc.sync.dma_start(sa_rows[:], sa.rearrange("(p t) o -> p (t o)", t=PACK))
         idx4 = load_list(offs4, "idx4")
         idx1 = load_list(offs, "idx1")
         xt_table = load_words(xt_words[0], U16, T, "xt_table")
         w_raw = load_words(w_words[0].rearrange("p n t -> p (n t)"), I32, R, "w_raw")
 
-        xo_plane = zeroed_plane(M, "xo_plane")
-        w2_plane_raw = zeroed_plane(R, "w2_plane_raw")
-        xt_plane = zeroed_plane(T, "xt_plane")
-        w_plane_raw = zeroed_plane(R, "w_plane_raw")
-        wb_plane = zeroed_plane(N, "wb_plane")
+        xo_plane = zeroed_plane(M, "xo_plane", "xo_plane", nc.vector)
+        w2_plane_raw = zeroed_plane(R, "w2_plane_raw", "w2_plane_raw", nc.vector)
         pv = [board("pv0", "pv0", nc.vector), board("pv1", "pv1")]
 
         spread_scales(xo_plane, xo_rows)
         spread_scales(w2_plane_raw, w2_rows)
         w2_plane = keep.tile([P, PACK, P], U8, name="w2_plane", align_bytes=64)
-        nc.vector.tensor_copy(w2_plane[:, :2, :], dealt(w2_plane_raw)[:, :2, :])
         w2_codes = keep.tile([P, PACK, P], U16, name="w2_codes", align_bytes=64)
         nc.scalar.copy(w2_codes[:], dealt(w2_raw))
-        xo_codes = keep.tile([P, J], U32, name="xo_codes", align_bytes=64)
-        xo_bytes = keep.tile([P, J], U8, name="xo_bytes", align_bytes=64)
+        sa_total = keep.tile([P, PACK], F32, name="sa_total")
+        nc.scalar.activation(sa_total[:], sa_rows[:], COPY, scale=float(C))
 
-        def product_b(t, lo, hi):
-            acc = psum.tile([P, J], F32, name="acc")
+        def gather_notes(table, dtype, lo, hi, name, tag):
+            picked = keep.tile([P, hi - lo], dtype, name=name, tag=tag, align_bytes=64)
+            nc.vector.tensor_copy(picked[:], table[:].indirect(entries(idx2, lo, hi)))
+            return picked
+
+        def product_b(acc, t, lo, hi, codes, scales):
             nc.tensor.matmul_mx(
                 acc[:, lo:hi], lhsT=w2_codes[:, t, :].bitcast(E2M1), lhsT_scale=w2_plane[:, t, :],
-                rhs=xo_codes[:, lo:hi].bitcast(E4M3), rhs_scale=xo_bytes[:, lo:hi], start=True, stop=True,
+                rhs=codes[:].bitcast(E4M3), rhs_scale=scales[:], start=True, stop=True,
             )
-            vals = keep.tile([P, hi - lo], F32, name="b%d_%d" % (t, lo), tag="b%d_%d" % (t, lo))
+
+        def put_b(acc, t, lo, hi):
+            vals = keep.tile([P, hi - lo], F32, name="b%d_%d" % (t, lo), tag="b%d_%d" % (t, lo), align_bytes=64)
             nc.vector.tensor_copy(vals[:], acc[:, lo:hi])
             scatter(pv[t], idx4, lo, hi, vals[:])
 
-        for lo, hi in ((0, 128), (128, 256), (256, 512)):
-            nc.vector.tensor_copy(xo_bytes[:, lo:hi], xo_plane[:].indirect(entries(idx2, lo, hi)))
-            nc.vector.tensor_copy(xo_codes[:, lo:hi], xo_table[:].indirect(entries(idx2, lo, hi)))
+        whole = {t: psum.tile([P, J], F32, name="acc") for t in (2, 3)}
+        for lo, hi, bytes_tag, words_tag in (
+            (0, 128, "xo_bytes", "xo_codes"), (128, 256, "sa_rows", "xo_codes_mid"), (256, 512, "xo_bytes", "xo_codes"),
+        ):
+            scales = gather_notes(xo_plane, U8, lo, hi, "xo_bytes%d" % lo, bytes_tag)
+            if lo == 0:
+                nc.vector.tensor_copy(w2_plane[:], dealt(w2_plane_raw))
+            codes = gather_notes(xo_table, U32, lo, hi, "xo_codes%d" % lo, words_tag)
             for t in range(2):
-                product_b(t, lo, hi)
-        nc.vector.tensor_copy(w2_plane[:, 2:, :], dealt(w2_plane_raw)[:, 2:, :])
+                acc = psum.tile([P, J], F32, name="acc")
+                product_b(acc, t, lo, hi, codes, scales)
+                put_b(acc, t, lo, hi)
+            for t in (2, 3):
+                product_b(whole[t], t, lo, hi, codes, scales)
+        xt_plane = zeroed_plane(T, "xt_plane", "b0_0", nc.gpsimd)
+        w_plane_raw = zeroed_plane(R, "w_plane_raw", "b1_0", nc.gpsimd)
         pv.append(board("pv2", "b0_128"))
-        product_b(2, 0, J)
+        put_b(whole[2], 2, 0, J)
         pv.append(board("pv3", "b0_256"))
-        product_b(3, 0, J)
+        put_b(whole[3], 3, 0, J)
+        wb_plane = zeroed_plane(N, "wb_plane", "b1_128", nc.gpsimd)
 
         load_scales(xt_plane, xt_scales)
         load_scales(w_plane_raw, w_scales)
         idx3 = load_list(offs3, "idx3")
-        sa_rows = keep.tile([P, PACK], F32, name="sa_rows")
-        nc.sync.dma_start(sa_rows[:], sa.rearrange("(p t) o -> p (t o)", t=PACK))
         idx5 = load_list(offs5, "idx5")
         wb_codes = load_words(wb_words[0], U16, N, "wb_codes")
         load_scales(wb_plane, wb_scales)
@@ -152,7 +165,7 @@ def tile_picked_tokens_bare_two_levelled_one_endsplit_kernel(
                 acc[:], lhsT=w_codes[:, t, :].bitcast(E4M3), lhsT_scale=w_plane[:, t, :],
                 rhs=xt_codes[:].bitcast(E2M1), rhs_scale=xt_bytes[:], start=True, stop=True,
             )
-            vals = keep.tile([P, J], F32, name="a%d" % t, tag="a%d" % t)
+            vals = keep.tile([P, J], F32, name="a%d" % t, tag="a%d" % t, align_bytes=64)
             nc.vector.tensor_copy(vals[:], acc[:])
             a_vals.append(vals)
         pw = []
@@ -169,7 +182,7 @@ def tile_picked_tokens_bare_two_levelled_one_endsplit_kernel(
             inv = keep.tile([P, 1], F32, name="inv%d" % t, tag="inv%d" % t)
             nc.vector.reciprocal(inv[:], total[:])
             q = keep.tile([P, 1], F32, name="ql%d" % t)
-            nc.vector.tensor_scalar(q[:], inv[:], sa_rows[:, t : t + 1], float(C), ALU.mult, ALU.mult)
+            nc.vector.tensor_scalar(q[:], inv[:], sa_total[:, t : t + 1], None, ALU.mult)
             pg.append(g)
             ql.append(q)
 
@@ -182,19 +195,17 @@ def tile_picked_tokens_bare_two_levelled_one_endsplit_kernel(
         hid_codes = keep.tile([P, O], U32, name="hid_codes", align_bytes=64)
         hid_bytes = keep.tile([P, O], U8, name="hid_bytes", align_bytes=64)
 
-        def quantise(planes, h):
-            woven = keep.tile([P, HALF, PACK], BF16, name="woven%d" % h, align_bytes=64)
+        def quantise(planes, lo, hi):
+            woven = keep.tile([P, hi - lo, PACK], BF16, name="woven%d" % lo, align_bytes=64)
             nc.vector.tensor_copy(
-                woven[:].rearrange("p (c i) t -> p c t i", i=4), planes[:].rearrange("p t (c i) -> p c t i", i=4)
+                woven[:].rearrange("p (c i) t -> p c t i", i=4), planes.rearrange("p t (c i) -> p c t i", i=4)
             )
-            cols = slice(h * HALF, (h + 1) * HALF)
-            nc.vector.quantize_mx(hid_codes[:, cols].bitcast(E4M3), hid_bytes[:, cols], woven[:].rearrange("p c t -> p (c t)"))
+            nc.vector.quantize_mx(hid_codes[:, lo:hi].bitcast(E4M3), hid_bytes[:, lo:hi], woven[:].rearrange("p c t -> p (c t)"))
 
-        def product_p(acc, u, h):
-            cols = slice(h * HALF, (h + 1) * HALF)
+        def product_p(acc, u, lo, hi):
             nc.tensor.matmul_mx(
-                acc[:, cols], lhsT=wb_codes[:, u * P : (u + 1) * P].bitcast(E2M1), lhsT_scale=wb_plane[:, u * P : (u + 1) * P],
-                rhs=hid_codes[:, cols].bitcast(E4M3), rhs_scale=hid_bytes[:, cols], start=True, stop=True,
+                acc[:, lo:hi], lhsT=wb_codes[:, u * P : (u + 1) * P].bitcast(E2M1), lhsT_scale=wb_plane[:, u * P : (u + 1) * P],
+                rhs=hid_codes[:, lo:hi].bitcast(E4M3), rhs_scale=hid_bytes[:, lo:hi], start=True, stop=True,
             )
 
         def split_and_scatter(acc, u, lo, hi):
@@ -205,21 +216,27 @@ def tile_picked_tokens_bare_two_levelled_one_endsplit_kernel(
             nc.vector.tensor_scalar(neg[:], acc[:, lo:hi], -1.0, 0.0, ALU.mult, ALU.max)
             scatter(m3[u], idx7, lo, hi, neg[:])
 
-        planes0 = keep.tile([P, PACK, HALF], BF16, name="planes0")
+        early = keep.tile([P, PACK + 1, HALF], BF16, name="early", tag="a%d" % (PACK - 1), align_bytes=64)
         for t in range(PACK):
-            fetch(planes0[:, t, :], t, 0)
-        planes1 = keep.tile([P, PACK, HALF], BF16, name="planes1", tag="inv%d" % (PACK - 1))
-        for t in range(PACK):
-            fetch(planes1[:, t, :], t, 1)
+            fetch(early[:, t, :], t, 0)
+        fetch(early[:, PACK, :], 0, 1)
+        late = keep.tile([P, PACK, HALF], BF16, name="late", tag="inv%d" % (PACK - 1))
+        for t in range(1, PACK):
+            fetch(late[:, t, :], t, 1)
 
-        last = psum.tile([P, O], F32, name="acc")
-        for h, planes in enumerate((planes0, planes1)):
-            quantise(planes, h)
+        quantise(early[:, :PACK, :128], 0, 128)
+        for u in range(2):
             acc = psum.tile([P, O], F32, name="acc")
-            product_p(acc, 0, h)
-            product_p(last, 1, h)
-            split_and_scatter(acc, 0, h * HALF, (h + 1) * HALF)
-        split_and_scatter(last, 1, 0, O)
+            product_p(acc, u, 0, 128)
+            split_and_scatter(acc, u, 0, 128)
+        quantise(early[:, :PACK, 128:], 128, HALF)
+        nc.vector.tensor_copy(late[:, 0, :], early[:, PACK, :])
+        quantise(late[:], HALF, O)
+        for u in range(2):
+            acc = psum.tile([P, O], F32, name="acc")
+            product_p(acc, u, 128, HALF)
+            product_p(acc, u, HALF, O)
+            split_and_scatter(acc, u, 128, O)
 
         def finish(u, lo, hi, queue):
             y = keep.tile([P, hi - lo], F32, name="y%d_%d" % (u, lo))

@@ -42,13 +42,17 @@ def tile_picked_tokens_bare_two_levelled_one_endsplit_kernel(
             return lst[:, lo // 16 : hi // 16]
 
         def load_words(src, dtype, width, name):
-            t = keep.tile([P, width], dtype, name=name, align_bytes=64)
+            t = keep.tile([P, width], dtype, name=name, tag=name, align_bytes=64)
             nc.sync.dma_start(t[:].bitcast(I32), src.bitcast(I32))
             return t
 
         def stage_scales(src, width, name):
-            rows = keep.tile([PACK, QUADS, width // 4], I32, name=name)
-            nc.sync.dma_start(rows[:], src[0].rearrange("(q i) n -> i q n", i=PACK).bitcast(I32))
+            rows = keep.tile([P, 2, width // 4], I32, name=name)
+            for half in range(2):
+                nc.sync.dma_start(
+                    rows[64 * half : 64 * half + PACK, :, :],
+                    src[0, 8 * half : 8 * half + 8, :].rearrange("(q i) n -> i q n", i=PACK).bitcast(I32),
+                )
             return rows
 
         def zeroed_plane(width, name, tag, engine):
@@ -58,7 +62,8 @@ def tile_picked_tokens_bare_two_levelled_one_endsplit_kernel(
 
         def spread_scales(plane, rows):
             for q in range(QUADS):
-                nc.vector.tensor_copy(plane[32 * q : 32 * q + PACK, :].bitcast(I32), rows[:, q, :])
+                first = 64 * (q // 2)
+                nc.vector.tensor_copy(plane[32 * q : 32 * q + PACK, :].bitcast(I32), rows[first : first + PACK, q % 2, :])
 
         def load_scales(plane, src):
             for q in range(QUADS):
@@ -83,9 +88,9 @@ def tile_picked_tokens_bare_two_levelled_one_endsplit_kernel(
         idx2 = load_list(offs2, "idx2")
         w2_raw = load_words(w2_words[0], U16, R, "w2_raw")
         xo_table = load_words(xo_words[0].rearrange("p n t -> p (n t)"), U32, M, "xo_table")
+        idx4 = load_list(offs4, "idx4")
         sa_rows = keep.tile([P, PACK], F32, name="sa_rows", tag="sa_rows", align_bytes=64)
         nc.sync.dma_start(sa_rows[:], sa.rearrange("(p t) o -> p (t o)", t=PACK))
-        idx4 = load_list(offs4, "idx4")
         idx1 = load_list(offs, "idx1")
         xt_table = load_words(xt_words[0], U16, T, "xt_table")
         w_raw = load_words(w_words[0].rearrange("p n t -> p (n t)"), I32, R, "w_raw")
@@ -101,6 +106,7 @@ def tile_picked_tokens_bare_two_levelled_one_endsplit_kernel(
         nc.scalar.copy(w2_codes[:], dealt(w2_raw))
         sa_total = keep.tile([P, PACK], F32, name="sa_total")
         nc.scalar.activation(sa_total[:], sa_rows[:], COPY, scale=float(C))
+        per_weight = keep.tile([P, PACK], F32, name="per_weight")
 
         def gather_notes(table, dtype, lo, hi, name, tag):
             picked = keep.tile([P, hi - lo], dtype, name=name, tag=tag, align_bytes=64)
@@ -115,7 +121,10 @@ def tile_picked_tokens_bare_two_levelled_one_endsplit_kernel(
 
         def put_b(acc, t, lo, hi):
             vals = keep.tile([P, hi - lo], F32, name="b%d_%d" % (t, lo), tag="b%d_%d" % (t, lo), align_bytes=64)
-            nc.vector.tensor_copy(vals[:], acc[:, lo:hi])
+            if (t, lo) == (0, 0):
+                nc.scalar.copy(vals[:], acc[:, lo:hi])
+            else:
+                nc.vector.tensor_copy(vals[:], acc[:, lo:hi])
             scatter(pv[t], idx4, lo, hi, vals[:])
 
         whole = {t: psum.tile([P, J], F32, name="acc") for t in (2, 3)}
@@ -132,13 +141,13 @@ def tile_picked_tokens_bare_two_levelled_one_endsplit_kernel(
                 put_b(acc, t, lo, hi)
             for t in (2, 3):
                 product_b(whole[t], t, lo, hi, codes, scales)
-        xt_plane = zeroed_plane(T, "xt_plane", "b0_0", nc.gpsimd)
-        w_plane_raw = zeroed_plane(R, "w_plane_raw", "b1_0", nc.gpsimd)
-        pv.append(board("pv2", "b0_128"))
+        w_plane_raw = zeroed_plane(R, "w_plane_raw", "xo_plane", nc.gpsimd)
+        xt_plane = zeroed_plane(T, "xt_plane", "xo_table", nc.gpsimd)
+        pv.append(board("pv2", "b1_128"))
         put_b(whole[2], 2, 0, J)
-        pv.append(board("pv3", "b0_256"))
+        wb_plane = zeroed_plane(N, "wb_plane", "b0_256", nc.gpsimd)
+        pv.append(board("pv3", "b1_256"))
         put_b(whole[3], 3, 0, J)
-        wb_plane = zeroed_plane(N, "wb_plane", "b1_128", nc.gpsimd)
 
         load_scales(xt_plane, xt_scales)
         load_scales(w_plane_raw, w_scales)
@@ -169,25 +178,29 @@ def tile_picked_tokens_bare_two_levelled_one_endsplit_kernel(
             nc.vector.tensor_copy(vals[:], acc[:])
             a_vals.append(vals)
         pw = []
-        for t, tag in enumerate(("b1_256", "b2_0", "b3_0", "a0")):
+        for t, tag in enumerate(("b2_0", "b3_0", "a0", "a1")):
             pw.append(board("pw%d" % t, tag))
             scatter(pw[t], idx3, 0, J, a_vals[t][:])
 
         pg, ql = [], []
+        nc.vector.reciprocal(per_weight[:], sa_total[:])
         for t in range(PACK):
             g = keep.tile([P, C], F32, name="pg%d" % t)
-            nc.vector.tensor_tensor(g[:], pw[t][:], pv[t][:], ALU.max)
-            total = keep.tile([P, 1], F32, name="total%d" % t)
-            nc.vector.tensor_reduce(total[:], g[:], mybir.AxisListType.X, ALU.add, apply_absolute_value=True)
+            total = keep.tile([P, 2], F32, name="total%d" % t)
+            halves = (slice(0, C // 2), slice(C // 2, C))
+            for cols in halves:
+                nc.vector.tensor_tensor(g[:, cols], pw[t][:, cols], pv[t][:, cols], ALU.max)
+            for i, cols in enumerate(halves):
+                nc.vector.tensor_reduce(total[:, i : i + 1], g[:, cols], mybir.AxisListType.X, ALU.add, apply_absolute_value=True)
             inv = keep.tile([P, 1], F32, name="inv%d" % t, tag="inv%d" % t)
-            nc.vector.reciprocal(inv[:], total[:])
+            nc.vector.tensor_scalar(inv[:], total[:, 0:1], total[:, 1:2], per_weight[:, t : t + 1], ALU.add, ALU.mult)
             q = keep.tile([P, 1], F32, name="ql%d" % t)
-            nc.vector.tensor_scalar(q[:], inv[:], sa_total[:, t : t + 1], None, ALU.mult)
+            nc.vector.reciprocal(q[:], inv[:])
             pg.append(g)
             ql.append(q)
 
         m2 = [board("m2_0", "pv0"), board("m2_1", "pv1")]
-        m3 = [board("m3_0", "b1_256"), board("m3_1", "b2_0")]
+        m3 = [board("m3_0", "b2_0"), board("m3_1", "b3_0")]
 
         def fetch(dst, t, h):
             nc.scalar.activation(dst, pg[t][:].indirect(entries(idx5, h * HALF, (h + 1) * HALF)), COPY, scale=ql[t][:])
@@ -210,7 +223,10 @@ def tile_picked_tokens_bare_two_levelled_one_endsplit_kernel(
 
         def split_and_scatter(acc, u, lo, hi):
             pos = keep.tile([P, hi - lo], F32, name="m0_%d_%d" % (u, lo))
-            nc.vector.tensor_scalar(pos[:], acc[:, lo:hi], 0.0, None, ALU.max)
+            if (u, lo) == (0, 0):
+                nc.scalar.activation(pos[:], acc[:, lo:hi], mybir.ActivationFunctionType.Relu)
+            else:
+                nc.vector.tensor_scalar(pos[:], acc[:, lo:hi], 0.0, None, ALU.max)
             scatter(m2[u], idx6, lo, hi, pos[:])
             neg = keep.tile([P, hi - lo], F32, name="m1_%d_%d" % (u, lo))
             nc.vector.tensor_scalar(neg[:], acc[:, lo:hi], -1.0, 0.0, ALU.mult, ALU.max)

@@ -202,8 +202,8 @@ def tile_picked_tokens_bare_two_levelled_one_endsplit_kernel(
         m2 = [board("m2_0", "pv0"), board("m2_1", "pv1")]
         m3 = [board("m3_0", "b2_0"), board("m3_1", "b3_0")]
 
-        def fetch(dst, t, h):
-            nc.scalar.activation(dst, pg[t][:].indirect(entries(idx5, h * HALF, (h + 1) * HALF)), COPY, scale=ql[t][:])
+        def fetch(dst, t, lo, hi):
+            nc.scalar.activation(dst, pg[t][:].indirect(entries(idx5, lo, hi)), COPY, scale=ql[t][:])
 
         hid_codes = keep.tile([P, O], U32, name="hid_codes", align_bytes=64)
         hid_bytes = keep.tile([P, O], U8, name="hid_bytes", align_bytes=64)
@@ -232,21 +232,21 @@ def tile_picked_tokens_bare_two_levelled_one_endsplit_kernel(
             nc.vector.tensor_scalar(neg[:], acc[:, lo:hi], -1.0, 0.0, ALU.mult, ALU.max)
             scatter(m3[u], idx7, lo, hi, neg[:])
 
-        early = keep.tile([P, PACK + 1, HALF], BF16, name="early", tag="a%d" % (PACK - 1), align_bytes=64)
-        for t in range(PACK):
-            fetch(early[:, t, :], t, 0)
-        fetch(early[:, PACK, :], 0, 1)
+        early = keep.tile([P, PACK, O], BF16, name="early", tag="a%d" % (PACK - 1), align_bytes=64)
+        fetch(early[:, 0, :], 0, 0, O)
+        for t in range(1, PACK):
+            fetch(early[:, t, :HALF], t, 0, HALF)
         late = keep.tile([P, PACK, HALF], BF16, name="late", tag="inv%d" % (PACK - 1))
         for t in range(1, PACK):
-            fetch(late[:, t, :], t, 1)
+            fetch(late[:, t, :], t, HALF, O)
 
-        quantise(early[:, :PACK, :128], 0, 128)
+        quantise(early[:, :, :128], 0, 128)
         for u in range(2):
             acc = psum.tile([P, O], F32, name="acc")
             product_p(acc, u, 0, 128)
             split_and_scatter(acc, u, 0, 128)
-        quantise(early[:, :PACK, 128:], 128, HALF)
-        nc.vector.tensor_copy(late[:, 0, :], early[:, PACK, :])
+        quantise(early[:, :, 128:HALF], 128, HALF)
+        nc.vector.tensor_copy(late[:, 0, :], early[:, 0, HALF:])
         quantise(late[:], HALF, O)
         for u in range(2):
             acc = psum.tile([P, O], F32, name="acc")
@@ -260,6 +260,5 @@ def tile_picked_tokens_bare_two_levelled_one_endsplit_kernel(
             queue.dma_start(out[u * P : (u + 1) * P, lo:hi], y[:])
 
         finish(0, 0, U, nc.sync)
-        finish(1, 0, 512, nc.sync)
-        finish(1, 512, 768, nc.scalar)
-        finish(1, 768, U, nc.sync)
+        for i in range(4):
+            finish(1, i * U // 4, (i + 1) * U // 4, nc.scalar if i % 2 else nc.sync)

from contextlib import ExitStack

import concourse.mybir as mybir

K, J, R, T, Z, M, C, O, N, U = 512, 512, 512, 2048, 512, 1024, 1024, 512, 256, 1024
FLOPS = 2 * K * R * J + 2 * Z * R * J + 2 * R * N * O

F32 = mybir.dt.float32
BF16 = mybir.dt.bfloat16
I32 = mybir.dt.int32
U32 = mybir.dt.uint32
U16 = mybir.dt.uint16
U8 = mybir.dt.uint8
E4M3 = mybir.dt.float8_e4m3fn_x4
E2M1 = mybir.dt.float4_e2m1fn_x4
ALU = mybir.AluOpType
COPY = mybir.ActivationFunctionType.Copy

P = 128
PACK = 4
QUADS = 4
HALF = O // 2


def tile_picked_tokens_bare_two_levelled_one_endsplit_kernel(
    tc, xt_words, xt_scales, w_words, w_scales, xo_words, xo_scales, w2_words, w2_scales, sa,
    wb_words, wb_scales, offs, offs2, offs3, offs4, offs5, offs6, offs7, out,
):
    nc = tc.nc

    with ExitStack() as ctx:
        lists = ctx.enter_context(tc.tile_pool(name="lists", bufs=1))
        keep = ctx.enter_context(tc.tile_pool(name="keep", bufs=1))
        psum = ctx.enter_context(tc.psum_pool(name="psum", bufs=8))

        def load_list(src, name):
            t = lists.tile([P, J // 16], U16, name=name)
            nc.sync.dma_start(t[:], src)
            return t

        def entries(lst, lo, hi):
            return lst[:, lo // 16 : hi // 16]

        def load_words(src, dtype, width, name):
            t = keep.tile([P, width], dtype, name=name, tag=name, align_bytes=64)
            nc.sync.dma_start(t[:].bitcast(I32), src.bitcast(I32))
            return t

        def stage_scales(src, width, name):
            rows = keep.tile([P, 2, width // 4], I32, name=name)
            for half in range(2):
                nc.sync.dma_start(
                    rows[64 * half : 64 * half + PACK, :, :],
                    src[0, 8 * half : 8 * half + 8, :].rearrange("(q i) n -> i q n", i=PACK).bitcast(I32),
                )
            return rows

        def zeroed_plane(width, name, tag, engine):
            plane = keep.tile([P, width], U8, name=name, tag=tag, align_bytes=64)
            engine.memset(plane[:].bitcast(I32), 0)
            return plane

        def spread_scales(plane, rows):
            for q in range(QUADS):
                first = 64 * (q // 2)
                nc.vector.tensor_copy(plane[32 * q : 32 * q + PACK, :].bitcast(I32), rows[first : first + PACK, q % 2, :])

        def load_scales(plane, src):
            for q in range(QUADS):
                nc.sync.dma_start(
                    plane[32 * q : 32 * q + PACK, :].bitcast(I32),
                    src[0, PACK * q : PACK * (q + 1), :].bitcast(I32),
                )

        def dealt(src):
            return src[:].rearrange("p (m t) -> p t m", t=PACK)

        def board(name, tag, engine=nc.gpsimd):
            t = keep.tile([P, C], F32, name=name, tag=tag, align_bytes=64)
            engine.memset(t[:], 0.0)
            return t

        def scatter(window, lst, lo, hi, values):
            nc.scalar.activation(window[:].indirect(entries(lst, lo, hi)), values, COPY)

        xo_rows = stage_scales(xo_scales, M, "xo_rows")
        w2_rows = stage_scales(w2_scales, R, "w2_rows")
        idx2 = load_list(offs2, "idx2")
        w2_raw = load_words(w2_words[0], U16, R, "w2_raw")
        xo_table = load_words(xo_words[0].rearrange("p n t -> p (n t)"), U32, M, "xo_table")
        idx4 = load_list(offs4, "idx4")
        sa_rows = keep.tile([P, PACK], F32, name="sa_rows", tag="sa_rows", align_bytes=64)
        nc.sync.dma_start(sa_rows[:], sa.rearrange("(p t) o -> p (t o)", t=PACK))
        idx1 = load_list(offs, "idx1")
        xt_table = load_words(xt_words[0], U16, T, "xt_table")
        w_raw = load_words(w_words[0].rearrange("p n t -> p (n t)"), I32, R, "w_raw")

        xo_plane = zeroed_plane(M, "xo_plane", "xo_plane", nc.vector)
        w2_plane_raw = zeroed_plane(R, "w2_plane_raw", "w2_plane_raw", nc.vector)
        pv = [board("pv0", "pv0", nc.vector), board("pv1", "pv1")]

        spread_scales(xo_plane, xo_rows)
        spread_scales(w2_plane_raw, w2_rows)
        w2_plane = keep.tile([P, PACK, P], U8, name="w2_plane", align_bytes=64)
        w2_codes = keep.tile([P, PACK, P], U16, name="w2_codes", align_bytes=64)
        nc.scalar.copy(w2_codes[:], dealt(w2_raw))
        sa_total = keep.tile([P, PACK], F32, name="sa_total")
        nc.scalar.activation(sa_total[:], sa_rows[:], COPY, scale=float(C))
        per_weight = keep.tile([P, PACK], F32, name="per_weight")

        def gather_notes(table, dtype, lo, hi, name, tag):
            picked = keep.tile([P, hi - lo], dtype, name=name, tag=tag, align_bytes=64)
            nc.vector.tensor_copy(picked[:], table[:].indirect(entries(idx2, lo, hi)))
            return picked

        def product_b(acc, t, lo, hi, codes, scales):
            nc.tensor.matmul_mx(
                acc[:, lo:hi], lhsT=w2_codes[:, t, :].bitcast(E2M1), lhsT_scale=w2_plane[:, t, :],
                rhs=codes[:].bitcast(E4M3), rhs_scale=scales[:], start=True, stop=True,
            )

        def put_b(acc, t, lo, hi):
            vals = keep.tile([P, hi - lo], F32, name="b%d_%d" % (t, lo), tag="b%d_%d" % (t, lo), align_bytes=64)
            if (t, lo) == (0, 0):
                nc.scalar.copy(vals[:], acc[:, lo:hi])
            else:
                nc.vector.tensor_copy(vals[:], acc[:, lo:hi])
            scatter(pv[t], idx4, lo, hi, vals[:])

        whole = {t: psum.tile([P, J], F32, name="acc") for t in (2, 3)}
        for lo, hi, bytes_tag, words_tag in (
            (0, 128, "xo_bytes", "xo_codes"), (128, 256, "sa_rows", "xo_codes_mid"), (256, 512, "xo_bytes", "xo_codes"),
        ):
            scales = gather_notes(xo_plane, U8, lo, hi, "xo_bytes%d" % lo, bytes_tag)
            if lo == 0:
                nc.vector.tensor_copy(w2_plane[:], dealt(w2_plane_raw))
            codes = gather_notes(xo_table, U32, lo, hi, "xo_codes%d" % lo, words_tag)
            for t in range(2):
                acc = psum.tile([P, J], F32, name="acc")
                product_b(acc, t, lo, hi, codes, scales)
                put_b(acc, t, lo, hi)
            for t in (2, 3):
                product_b(whole[t], t, lo, hi, codes, scales)
        w_plane_raw = zeroed_plane(R, "w_plane_raw", "xo_plane", nc.gpsimd)
        xt_plane = zeroed_plane(T, "xt_plane", "xo_table", nc.gpsimd)
        pv.append(board("pv2", "b1_128"))
        put_b(whole[2], 2, 0, J)
        wb_plane = zeroed_plane(N, "wb_plane", "b0_256", nc.gpsimd)
        pv.append(board("pv3", "b1_256"))
        put_b(whole[3], 3, 0, J)

        load_scales(xt_plane, xt_scales)
        load_scales(w_plane_raw, w_scales)
        idx3 = load_list(offs3, "idx3")
        idx5 = load_list(offs5, "idx5")
        wb_codes = load_words(wb_words[0], U16, N, "wb_codes")
        load_scales(wb_plane, wb_scales)
        idx6 = load_list(offs6, "idx6")
        idx7 = load_list(offs7, "idx7")

        w_codes = keep.tile([P, PACK, P], I32, name="w_codes", align_bytes=64)
        nc.vector.tensor_copy(w_codes[:], dealt(w_raw))
        w_plane = keep.tile([P, PACK, P], U8, name="w_plane", align_bytes=64)
        nc.vector.tensor_copy(w_plane[:], dealt(w_plane_raw))
        xt_codes = keep.tile([P, J], U16, name="xt_codes", align_bytes=64)
        nc.vector.tensor_copy(xt_codes[:], xt_table[:].indirect(idx1[:]))
        xt_bytes = keep.tile([P, J], U8, name="xt_bytes", align_bytes=64)
        nc.vector.tensor_copy(xt_bytes[:], xt_plane[:].indirect(idx1[:]))

        a_vals = []
        for t in range(PACK):
            acc = psum.tile([P, J], F32, name="acc")
            nc.tensor.matmul_mx(
                acc[:], lhsT=w_codes[:, t, :].bitcast(E4M3), lhsT_scale=w_plane[:, t, :],
                rhs=xt_codes[:].bitcast(E2M1), rhs_scale=xt_bytes[:], start=True, stop=True,
            )
            vals = keep.tile([P, J], F32, name="a%d" % t, tag="a%d" % t, align_bytes=64)
            nc.vector.tensor_copy(vals[:], acc[:])
            a_vals.append(vals)
        pw = []
        for t, tag in enumerate(("b2_0", "b3_0", "a0", "a1")):
            pw.append(board("pw%d" % t, tag))
            scatter(pw[t], idx3, 0, J, a_vals[t][:])

        pg, ql = [], []
        nc.vector.reciprocal(per_weight[:], sa_total[:])
        for t in range(PACK):
            g = keep.tile([P, C], F32, name="pg%d" % t)
            total = keep.tile([P, 2], F32, name="total%d" % t)
            halves = (slice(0, C // 2), slice(C // 2, C))
            for cols in halves:
                nc.vector.tensor_tensor(g[:, cols], pw[t][:, cols], pv[t][:, cols], ALU.max)
            for i, cols in enumerate(halves):
                nc.vector.tensor_reduce(total[:, i : i + 1], g[:, cols], mybir.AxisListType.X, ALU.add, apply_absolute_value=True)
            inv = keep.tile([P, 1], F32, name="inv%d" % t, tag="inv%d" % t)
            nc.vector.tensor_scalar(inv[:], total[:, 0:1], total[:, 1:2], per_weight[:, t : t + 1], ALU.add, ALU.mult)
            q = keep.tile([P, 1], F32, name="ql%d" % t)
            nc.vector.reciprocal(q[:], inv[:])
            pg.append(g)
            ql.append(q)

        m2 = [board("m2_0", "pv0"), board("m2_1", "pv1")]
        m3 = [board("m3_0", "b2_0"), board("m3_1", "b3_0")]

        def fetch(dst, t, lo, hi):
            nc.scalar.activation(dst, pg[t][:].indirect(entries(idx5, lo, hi)), COPY, scale=ql[t][:])

        hid_codes = keep.tile([P, O], U32, name="hid_codes", align_bytes=64)
        hid_bytes = keep.tile([P, O], U8, name="hid_bytes", align_bytes=64)

        def quantise(planes, lo, hi):
            woven = keep.tile([P, hi - lo, PACK], BF16, name="woven%d" % lo, align_bytes=64)
            nc.vector.tensor_copy(
                woven[:].rearrange("p (c i) t -> p c t i", i=4), planes.rearrange("p t (c i) -> p c t i", i=4)
            )
            nc.vector.quantize_mx(hid_codes[:, lo:hi].bitcast(E4M3), hid_bytes[:, lo:hi], woven[:].rearrange("p c t -> p (c t)"))

        def product_p(acc, u, lo, hi):
            nc.tensor.matmul_mx(
                acc[:, lo:hi], lhsT=wb_codes[:, u * P : (u + 1) * P].bitcast(E2M1), lhsT_scale=wb_plane[:, u * P : (u + 1) * P],
                rhs=hid_codes[:, lo:hi].bitcast(E4M3), rhs_scale=hid_bytes[:, lo:hi], start=True, stop=True,
            )

        def split_and_scatter(acc, u, lo, hi):
            pos = keep.tile([P, hi - lo], F32, name="m0_%d_%d" % (u, lo))
            if (u, lo) == (0, 0):
                nc.scalar.activation(pos[:], acc[:, lo:hi], mybir.ActivationFunctionType.Relu)
            else:
                nc.vector.tensor_scalar(pos[:], acc[:, lo:hi], 0.0, None, ALU.max)
            scatter(m2[u], idx6, lo, hi, pos[:])
            neg = keep.tile([P, hi - lo], F32, name="m1_%d_%d" % (u, lo))
            nc.vector.tensor_scalar(neg[:], acc[:, lo:hi], -1.0, 0.0, ALU.mult, ALU.max)
            scatter(m3[u], idx7, lo, hi, neg[:])

        early = keep.tile([P, PACK, O], BF16, name="early", tag="a%d" % (PACK - 1), align_bytes=64)
        fetch(early[:, 0, :], 0, 0, O)
        for t in range(1, PACK):
            fetch(early[:, t, :HALF], t, 0, HALF)
        late = keep.tile([P, PACK, HALF], BF16, name="late", tag="inv%d" % (PACK - 1))
        for t in range(1, PACK):
            fetch(late[:, t, :], t, HALF, O)

        quantise(early[:, :, :128], 0, 128)
        for u in range(2):
            acc = psum.tile([P, O], F32, name="acc")
            product_p(acc, u, 0, 128)
            split_and_scatter(acc, u, 0, 128)
        quantise(early[:, :, 128:HALF], 128, HALF)
        nc.vector.tensor_copy(late[:, 0, :], early[:, 0, HALF:])
        quantise(late[:], HALF, O)
        for u in range(2):
            acc = psum.tile([P, O], F32, name="acc")
            product_p(acc, u, 128, HALF)
            product_p(acc, u, HALF, O)
            split_and_scatter(acc, u, 128, O)

        def finish(u, lo, hi, queue):
            y = keep.tile([P, hi - lo], F32, name="y%d_%d" % (u, lo))
            nc.vector.tensor_tensor(y[:], m2[u][:, lo:hi], m3[u][:, lo:hi], ALU.subtract)
            queue.dma_start(out[u * P : (u + 1) * P, lo:hi], y[:])

        finish(0, 0, U, nc.sync)
        for i in range(4):
            finish(1, i * U // 4, (i + 1) * U // 4, nc.scalar if i % 2 else nc.sync)
